import numpy as np
import ml_dtypes


def mxq(x, axis, fmt="e4m3"):
    dtype, down = {"e4m3": (ml_dtypes.float8_e4m3fn, 7), "e5m2": (ml_dtypes.float8_e5m2, 14)}[fmt]
    v = np.moveaxis(np.asarray(x, np.float32).astype(ml_dtypes.bfloat16).astype(np.float64), axis, -1)
    blocks = v.reshape(v.shape[:-1] + (-1, 32))
    amax = np.abs(blocks).max(-1, keepdims=True)
    byte = np.maximum(np.where(amax > 0, np.frexp(amax)[1] - 1 + 127, 0) - down, 1)
    scale = np.exp2(byte - 127.0)
    codes = (blocks / scale).astype(np.float32).astype(dtype).astype(np.float64)
    return np.moveaxis((codes * scale).reshape(v.shape), -1, axis)


WIDE = False


def mx_kscale(k):
    if not WIDE:
        return np.ones(k)
    levels = np.array([10, -10, 5, -5, 0])
    if k % 512:
        return np.exp2(np.random.permutation(np.resize(levels, k // 32))).repeat(32)
    a = np.empty((k // 512, 16))
    for p in range(k // 512):
        a[p, :8] = np.random.permutation(np.resize(levels, 8))
        for g in range(8):
            far = levels[np.abs(levels - a[p, g]) >= 10]
            a[p, g + 8] = far[np.random.randint(len(far))]
    return np.exp2(a.ravel()).repeat(32)


def f64(x):
    return np.asarray(x).astype(np.float64)


def striped(idx):
    return np.tile(idx.reshape(-1, 16).T, (8, 1)).astype(np.uint16)


def unstriped(offs):
    return offs[:16].T.reshape(-1).astype(np.int64)


def striped8(idx):
    return np.concatenate([x.reshape(-1, 16).T for x in idx]).astype(np.uint16)


def runs(offs, k):
    lists = np.stack([offs[16 * r : 16 * r + 16].T.reshape(-1) for r in range(8)]).astype(np.int64)
    return lists[np.arange(k) % 512 // 64]


def pack_weight(w):
    k, n = w.shape
    w = f64(np.asarray(w, np.float32).astype(ml_dtypes.bfloat16)).reshape(k // 32, 32, n)
    amax = np.abs(w).max(1)
    byte = np.clip(np.where(amax > 0, np.frexp(amax)[1] - 1 + 127 - 7, 1), 1, 254)
    scaled = (w * np.exp2(127.0 - byte)[:, None, :]).reshape(k, n).astype(np.float32)
    words = np.ascontiguousarray(scaled.reshape(k // 512, 128, 4, n).transpose(0, 1, 3, 2)).astype(ml_dtypes.float8_e4m3fn).view(np.uint8)
    return words, np.ascontiguousarray(byte.astype(np.uint8).reshape(k // 512, 16, n))


def unpack_weight(words, scales):
    g, p, n, _ = words.shape
    vals = np.ascontiguousarray(words).view(ml_dtypes.float8_e4m3fn).astype(np.float64) * np.repeat(np.exp2(scales.astype(np.float64) - 127.0), 8, axis=1)[..., None]
    return vals.transpose(0, 1, 3, 2).reshape(g * 512, n)


K, T, S, N, H = 512, 2048, 512, 512, 512


def setup_inputs():
    n = np.random.standard_normal
    s = mx_kscale(K)[:, None]
    u = mx_kscale(S)
    packed_xT = pack_weight(n((K, T)) * s)
    return {
        "x_words": packed_xT[0],
        "x_scales": packed_xT[1],
        "wa": (n((K, H)) / np.sqrt(K) / s).astype(np.float32),
        "gt": (np.random.uniform(0.5, 1.5, (S, 1)) * u[:, None]).astype(np.float32),
        "w1": (n((S, N)) / np.sqrt(S) / u[:, None]).astype(np.float32),
        "offs": striped(np.random.permutation(T)[:S]),
        "n1": striped8(np.stack([np.random.permutation(H) for _ in range(8)])),
        "n2": striped8(np.stack([np.random.permutation(H) for _ in range(8)])),
        "n3": striped8(np.stack([np.random.permutation(H) for _ in range(8)])),
        "n4": striped8(np.stack([np.random.permutation(H) for _ in range(8)])),
    }


def reference(x_words, x_scales, wa, gt, w1, offs, n1, n2, n3, n4):
    xq = unpack_weight(x_words, x_scales)[:, unstriped(offs)]
    y = xq.T @ mxq(f64(wa), 0, "e4m3")
    st = y + y[np.arange(S)[:, None], runs(n1, S)]
    z = f64(gt) * (st * (np.tanh(st[np.arange(S)[:, None], runs(n2, S)])))
    h = mxq(f64(w1), 0, "e4m3").T @ mxq(z, 0, "e4m3")
    pa = h[np.arange(N)[:, None], runs(n3, N)]
    pb = h[np.arange(N)[:, None], runs(n4, N)]
    return np.maximum(np.maximum(h, pa), pb) - (0.5 * (np.minimum(np.minimum(h, pa), pb)))

@@ -1,0 +1,167 @@
+from contextlib import ExitStack
+
+import concourse.mybir as mybir
+
+K, T, S, N, H = 512, 2048, 512, 512, 512
+FLOPS = 2 * K * S * H + 2 * S * N * H
+
+F32 = mybir.dt.float32
+BF16 = mybir.dt.bfloat16
+I32 = mybir.dt.int32
+U32 = mybir.dt.uint32
+U16 = mybir.dt.uint16
+U8 = mybir.dt.uint8
+FP8X4 = mybir.dt.float8_e4m3fn_x4
+ALU = mybir.AluOpType
+ACT = mybir.ActivationFunctionType
+
+P = 128
+PACK = 4
+HALF = 256
+
+
+def tile_picked_tokhopprange_none_p_kernel(
+    tc, x_words, x_scales, wa, gt, w1, offs, n1, n2, n3, n4, out
+):
+    nc = tc.nc
+    with ExitStack() as ctx:
+        keep = ctx.enter_context(tc.tile_pool(name="keep", bufs=1))
+        psum = ctx.enter_context(tc.psum_pool(name="psum", bufs=1))
+
+        def list_tile(name):
+            return keep.tile([P, S // 16], U16, name=name)
+
+        offs_sb, n1_sb, n2_sb, n3_sb, n4_sb = [list_tile(nm) for nm in ("offs_sb", "n1_sb", "n2_sb", "n3_sb", "n4_sb")]
+
+        xs = keep.tile([P, T], U8, name="xs", align_bytes=64)
+        xw = keep.tile([P, T], U32, name="xw", align_bytes=64)
+        nc.vector.memset(xs[:].bitcast(I32), 0)
+        warm_in = keep.tile([P, 1], F32, name="warm_in")
+        warm_out = keep.tile([P, 1], F32, name="warm_out")
+        nc.vector.memset(warm_in[:], 0.0)
+        nc.scalar.activation(warm_out[:], warm_in[:], ACT.Tanh)
+
+        nc.sync.dma_start(offs_sb[:], offs)
+        nc.sync.dma_start(xw[:].bitcast(I32), x_words[0].rearrange("p c r -> p (c r)").bitcast(I32))
+        for q in range(4):
+            nc.sync.dma_start(xs[32 * q : 32 * q + 4, :].bitcast(I32), x_scales[0, 4 * q : 4 * q + 4, :].bitcast(I32))
+        wa_rows = wa.rearrange("(p j) c -> p j c", j=PACK)
+        wa_raw = [keep.tile([P, PACK, HALF], F32, name=f"wa_raw{a}") for a in range(2)]
+        for a in range(2):
+            nc.sync.dma_start(wa_raw[a][:], wa_rows[:, :, a * HALF : (a + 1) * HALF])
+        nc.sync.dma_start(n1_sb[:], n1)
+        gt_sb = keep.tile([P, PACK], F32, name="gt_sb")
+        nc.sync.dma_start(gt_sb[:], gt.rearrange("(p t) o -> p (t o)", t=PACK))
+        nc.sync.dma_start(n2_sb[:], n2)
+        w1_raw = keep.tile([P, PACK, N], F32, name="w1_raw")
+        nc.sync.dma_start(w1_raw[:], w1.rearrange("(p j) c -> p j c", j=PACK))
+        nc.sync.dma_start(n3_sb[:], n3)
+        nc.sync.dma_start(n4_sb[:], n4)
+
+        win = [keep.tile([P, 2 * H], F32, name=f"win{t}") for t in range(PACK)]
+        for t in range(PACK):
+            nc.gpsimd.memset(win[t][:, H:], 0.0)
+
+        gs = keep.tile([P, S], U8, name="gs", align_bytes=64)
+        gw = keep.tile([P, S], U32, name="gw", align_bytes=64)
+        ds = keep.tile([P, S], U8, name="ds", align_bytes=64)
+        dw = keep.tile([P, S], U32, name="dw", align_bytes=64)
+        nc.vector.tensor_copy(gs[:], xs[:].indirect(offs_sb[:]))
+        nc.vector.tensor_copy(gw[:], xw[:].indirect(offs_sb[:]))
+        nc.vector.tensor_copy(ds[:].rearrange("p (t m) -> p t m", t=PACK), gs[:].rearrange("p (m t) -> p t m", t=PACK))
+        nc.vector.tensor_copy(
+            dw[:].bitcast(I32).rearrange("p (t m) -> p t m", t=PACK),
+            gw[:].bitcast(I32).rearrange("p (m t) -> p t m", t=PACK),
+        )
+
+        def interleave(engine_copy, dst, src):
+            engine_copy(
+                dst.rearrange("p (c i) t -> p c t i", i=4),
+                src.rearrange("p t (c i) -> p c t i", i=4),
+            )
+
+        wa_codes = keep.tile([P, H], U32, name="wa_codes", align_bytes=64)
+        wa_scales = keep.tile([P, H], U8, name="wa_scales", align_bytes=64)
+        for a in range(2):
+            wa_bf = keep.tile([P, HALF, PACK], BF16, name=f"wa_bf{a}", align_bytes=64)
+            interleave(nc.scalar.copy if a == 0 else nc.vector.tensor_copy, wa_bf[:], wa_raw[a][:])
+            cols = slice(a * HALF, (a + 1) * HALF)
+            nc.vector.quantize_mx(
+                out=wa_codes[:, cols].bitcast(FP8X4), scales=wa_scales[:, cols], in_=wa_bf[:].rearrange("p c j -> p (c j)")
+            )
+
+        y_ps = [psum.tile([P, H], F32, name=f"y_ps{t}") for t in range(PACK)]
+        plain = [keep.tile([P, H], F32, name=f"plain{t}") for t in range(PACK)]
+        st = [keep.tile([P, H], F32, name=f"st{t}") for t in range(PACK)]
+        th = [keep.tile([P, H], F32, name=f"th{t}") for t in range(PACK)]
+        for t in range(PACK):
+            rows = slice(t * P, (t + 1) * P)
+            nc.tensor.matmul_mx(
+                out=y_ps[t][:], lhsT=dw[:, rows].bitcast(FP8X4), lhsT_scale=ds[:, rows],
+                rhs=wa_codes[:].bitcast(FP8X4), rhs_scale=wa_scales[:], start=True, stop=True,
+            )
+            nc.scalar.copy(win[t][:, :H], y_ps[t][:])
+            nc.scalar.copy(plain[t][:], y_ps[t][:])
+            nc.vector.tensor_tensor(st[t][:], win[t][:].indirect(n1_sb[:]), plain[t][:], ALU.add)
+        for t in range(PACK):
+            nc.scalar.activation(th[t][:], st[t][:], ACT.Tanh)
+
+        gated = [keep.tile([P, HALF], F32, name=f"gated{b}") for b in range(2)]
+        z4 = [keep.tile([P, PACK, HALF], F32, name=f"z4_{a}") for a in range(2)]
+        for a in range(2):
+            cols = slice(a * HALF, (a + 1) * HALF)
+            for t in range(PACK):
+                g = gated[t % 2]
+                nc.scalar.activation(g[:], st[t][:, cols], ACT.Copy, scale=gt_sb[:, t : t + 1])
+                nc.vector.tensor_tensor(
+                    z4[a][:, t, :], th[t][:].indirect(n2_sb[:, a * 16 : (a + 1) * 16]), g[:], ALU.mult
+                )
+
+        w1_bf = keep.tile([P, PACK, P, PACK], BF16, name="w1_bf", align_bytes=64)
+        w1_src = w1_raw[:].rearrange("p j (m t) -> p m t j", t=PACK)
+        w1_dst = w1_bf[:].rearrange("p t m j -> p m t j")
+        for q in range(4):
+            nc.scalar.copy(w1_dst[:, 32 * q : 32 * q + 32], w1_src[:, 32 * q : 32 * q + 32])
+        w1_codes = keep.tile([P, N], U32, name="w1_codes", align_bytes=64)
+        w1_scales = keep.tile([P, N], U8, name="w1_scales", align_bytes=64)
+        nc.vector.quantize_mx(
+            out=w1_codes[:].bitcast(FP8X4), scales=w1_scales[:], in_=w1_bf[:].rearrange("p t m j -> p (t m j)")
+        )
+
+        h_ps = [psum.tile([P, H], F32, name=f"h_ps{t}") for t in range(PACK)]
+        for a in range(2):
+            cols = slice(a * HALF, (a + 1) * HALF)
+            z_bf = keep.tile([P, HALF, PACK], BF16, name=f"z_bf{a}", align_bytes=64)
+            if a == 0:
+                interleave(nc.scalar.copy, z_bf[:], z4[a][:])
+            else:
+                interleave(nc.vector.tensor_copy, z_bf[:, :160, :], z4[a][:, :, :160])
+                interleave(nc.scalar.copy, z_bf[:, 160:, :], z4[a][:, :, 160:])
+            z_codes = keep.tile([P, HALF], U32, name=f"z_codes{a}", align_bytes=64)
+            z_scales = keep.tile([P, HALF], U8, name=f"z_scales{a}", align_bytes=64)
+            nc.vector.quantize_mx(
+                out=z_codes[:].bitcast(FP8X4), scales=z_scales[:], in_=z_bf[:].rearrange("p c j -> p (c j)")
+            )
+            for t in range(PACK):
+                rows = slice(t * P, (t + 1) * P)
+                nc.tensor.matmul_mx(
+                    out=h_ps[t][:, cols], lhsT=w1_codes[:, rows].bitcast(FP8X4), lhsT_scale=w1_scales[:, rows],
+                    rhs=z_codes[:].bitcast(FP8X4), rhs_scale=z_scales[:], start=True, stop=True,
+                )
+                nc.scalar.copy(win[t][:, cols], h_ps[t][:, cols])
+                nc.scalar.copy(plain[t][:, cols], h_ps[t][:, cols])
+
+        out_rows = out.rearrange("(p t) j -> p t j", t=PACK)
+        for t in range(PACK):
+            d1, d2 = st[t], th[t]
+            hi = keep.tile([P, H], F32, name=f"hi{t}")
+            lo = keep.tile([P, H], F32, name=f"lo{t}")
+            mid = keep.tile([P, H], F32, name=f"mid{t}")
+            res = keep.tile([P, H], F32, name=f"res{t}")
+            nc.vector.tensor_tensor(d1[:], win[t][:].indirect(n3_sb[:]), plain[t][:], ALU.subtract)
+            nc.vector.tensor_tensor(d2[:], win[t][:].indirect(n4_sb[:]), plain[t][:], ALU.subtract)
+            nc.vector.scalar_tensor_tensor(hi[:], d1[:], 0.0, d2[:], ALU.max, ALU.max)
+            nc.vector.scalar_tensor_tensor(lo[:], d1[:], 0.0, d2[:], ALU.min, ALU.min)
+            nc.vector.scalar_tensor_tensor(mid[:], h_ps[t][:], 0.5, hi[:], ALU.mult, ALU.add)
+            nc.vector.scalar_tensor_tensor(res[:], lo[:], -0.5, mid[:], ALU.mult, ALU.add)
+            nc.sync.dma_start(out_rows[:, t, :], res[:])

@@ -1,6 +1,7 @@
 from contextlib import ExitStack
 
 import concourse.mybir as mybir
+from concourse.masks import make_identity
 
 K, T, S, N, H = 512, 2048, 512, 512, 512
 FLOPS = 2 * K * S * H + 2 * S * N * H
@@ -33,25 +34,25 @@ def tile_picked_tokhopprange_none_p_kernel(
 
         offs_sb, n1_sb, n2_sb, n3_sb, n4_sb = [list_tile(nm) for nm in ("offs_sb", "n1_sb", "n2_sb", "n3_sb", "n4_sb")]
 
-        xs = keep.tile([P, T], U8, name="xs", align_bytes=64)
+        xs = keep.tile([P, T], U8, name="xs", tag="xs", align_bytes=64)
         xw = keep.tile([P, T], U32, name="xw", align_bytes=64)
-        nc.vector.memset(xs[:].bitcast(I32), 0)
+        nc.gpsimd.memset(xs[:].bitcast(I32), 0)
         warm_in = keep.tile([P, 1], F32, name="warm_in")
         warm_out = keep.tile([P, 1], F32, name="warm_out")
         nc.vector.memset(warm_in[:], 0.0)
         nc.scalar.activation(warm_out[:], warm_in[:], ACT.Tanh)
 
         nc.sync.dma_start(offs_sb[:], offs)
-        nc.sync.dma_start(xw[:].bitcast(I32), x_words[0].rearrange("p c r -> p (c r)").bitcast(I32))
-        for q in range(4):
-            nc.sync.dma_start(xs[32 * q : 32 * q + 4, :].bitcast(I32), x_scales[0, 4 * q : 4 * q + 4, :].bitcast(I32))
         wa_rows = wa.rearrange("(p j) c -> p j c", j=PACK)
-        wa_raw = [keep.tile([P, PACK, HALF], F32, name=f"wa_raw{a}") for a in range(2)]
-        for a in range(2):
-            nc.sync.dma_start(wa_raw[a][:], wa_rows[:, :, a * HALF : (a + 1) * HALF])
-        nc.sync.dma_start(n1_sb[:], n1)
+        wa_raw = [keep.tile([P, PACK, HALF], F32, name=f"wa_raw{a}", tag=f"wa_raw{a}") for a in range(2)]
+        nc.sync.dma_start(wa_raw[0][:], wa_rows[:, :, :HALF])
+        for q in range(4):
+            nc.sync.dma_start(xs[q:P:32, :].bitcast(I32), x_scales[0, q:16:4, :].bitcast(I32))
+        nc.sync.dma_start(xw[:].bitcast(I32), x_words[0].rearrange("p c r -> p (c r)").bitcast(I32))
+        nc.sync.dma_start(wa_raw[1][:], wa_rows[:, :, HALF:])
         gt_sb = keep.tile([P, PACK], F32, name="gt_sb")
         nc.sync.dma_start(gt_sb[:], gt.rearrange("(p t) o -> p (t o)", t=PACK))
+        nc.sync.dma_start(n1_sb[:], n1)
         nc.sync.dma_start(n2_sb[:], n2)
         w1_raw = keep.tile([P, PACK, N], F32, name="w1_raw")
         nc.sync.dma_start(w1_raw[:], w1.rearrange("(p j) c -> p j c", j=PACK))
@@ -62,17 +63,13 @@ def tile_picked_tokhopprange_none_p_kernel(
         for t in range(PACK):
             nc.gpsimd.memset(win[t][:, H:], 0.0)
 
+        ident = keep.tile([P, P], F32, name="ident")
+        make_identity(nc, ident[:])
+
         gs = keep.tile([P, S], U8, name="gs", align_bytes=64)
         gw = keep.tile([P, S], U32, name="gw", align_bytes=64)
         ds = keep.tile([P, S], U8, name="ds", align_bytes=64)
-        dw = keep.tile([P, S], U32, name="dw", align_bytes=64)
-        nc.vector.tensor_copy(gs[:], xs[:].indirect(offs_sb[:]))
-        nc.vector.tensor_copy(gw[:], xw[:].indirect(offs_sb[:]))
-        nc.vector.tensor_copy(ds[:].rearrange("p (t m) -> p t m", t=PACK), gs[:].rearrange("p (m t) -> p t m", t=PACK))
-        nc.vector.tensor_copy(
-            dw[:].bitcast(I32).rearrange("p (t m) -> p t m", t=PACK),
-            gw[:].bitcast(I32).rearrange("p (m t) -> p t m", t=PACK),
-        )
+        dw0 = keep.tile([P, P], U32, name="dw0", align_bytes=64)
 
         def interleave(engine_copy, dst, src):
             engine_copy(
@@ -80,88 +77,173 @@ def tile_picked_tokhopprange_none_p_kernel(
                 src.rearrange("p t (c i) -> p c t i", i=4),
             )
 
-        wa_codes = keep.tile([P, H], U32, name="wa_codes", align_bytes=64)
         wa_scales = keep.tile([P, H], U8, name="wa_scales", align_bytes=64)
-        for a in range(2):
-            wa_bf = keep.tile([P, HALF, PACK], BF16, name=f"wa_bf{a}", align_bytes=64)
-            interleave(nc.scalar.copy if a == 0 else nc.vector.tensor_copy, wa_bf[:], wa_raw[a][:])
-            cols = slice(a * HALF, (a + 1) * HALF)
-            nc.vector.quantize_mx(
-                out=wa_codes[:, cols].bitcast(FP8X4), scales=wa_scales[:, cols], in_=wa_bf[:].rearrange("p c j -> p (c j)")
-            )
+        wa_bf = [keep.tile([P, HALF, PACK], BF16, name=f"wa_bf{a}", tag=f"wa_bf{a}", align_bytes=64) for a in range(2)]
 
-        y_ps = [psum.tile([P, H], F32, name=f"y_ps{t}") for t in range(PACK)]
+        def quantize(codes, scales, bf):
+            nc.vector.quantize_mx(out=codes.bitcast(FP8X4), scales=scales, in_=bf.rearrange("p c j -> p (c j)"))
+
+        interleave(nc.scalar.copy, wa_bf[0][:], wa_raw[0][:])
+        nc.vector.tensor_copy(gs[:], xs[:].indirect(offs_sb[:]))
+        wa_codes = keep.tile([P, H], U32, name="wa_codes", tag="xs", align_bytes=64)
+        quantize(wa_codes[:, :HALF], wa_scales[:, :HALF], wa_bf[0][:])
+        nc.vector.tensor_copy(ds[:].rearrange("p (t m) -> p t m", t=PACK), gs[:].rearrange("p (m t) -> p t m", t=PACK))
+        nc.vector.tensor_copy(gw[:], xw[:].indirect(offs_sb[:]))
+        gw_by_tile = gw[:].bitcast(I32).rearrange("p (m t) -> p t m", t=PACK)
+        nc.vector.tensor_copy(dw0[:].bitcast(I32), gw_by_tile[:, 0, :])
+        interleave(nc.vector.tensor_copy, wa_bf[1][:, :P, :], wa_raw[1][:, :, :P])
+        interleave(nc.scalar.copy, wa_bf[1][:, P:, :], wa_raw[1][:, :, P:])
+        quantize(wa_codes[:, HALF:], wa_scales[:, HALF:], wa_bf[1][:])
+        dw_rest = keep.tile([P, PACK - 1, P], U32, name="dw_rest", tag="wa_bf1", align_bytes=64)
+        nc.vector.tensor_copy(dw_rest[:].bitcast(I32), gw_by_tile[:, 1:, :])
+        dw = [dw0[:]] + [dw_rest[:, t, :] for t in range(PACK - 1)]
+
+        gt_safe = keep.tile([P, PACK], F32, name="gt_safe", tag="wa_raw1")
+        gt_rec = keep.tile([P, PACK], F32, name="gt_rec")
+        gt_inv = keep.tile([P, PACK], F32, name="gt_inv")
+        nc.vector.scalar_tensor_tensor(gt_safe[:], gt_sb[:], 0.0, gt_sb[:], ALU.is_equal, ALU.add)
+        nc.vector.reciprocal(gt_rec[:], gt_safe[:])
+        nc.vector.tensor_scalar(gt_inv[:], gt_rec[:], 3.0e38, -3.0e38, ALU.min, ALU.max)
+
+        bank = [psum.tile([P, H], F32, name=f"bank{b}") for b in range(8)]
         plain = [keep.tile([P, H], F32, name=f"plain{t}") for t in range(PACK)]
+        y_plain = plain[: PACK - 1] + [keep.tile([P, H], F32, name="y_plain3", tag="late", align_bytes=64)]
         st = [keep.tile([P, H], F32, name=f"st{t}") for t in range(PACK)]
         th = [keep.tile([P, H], F32, name=f"th{t}") for t in range(PACK)]
-        for t in range(PACK):
+
+        def y_product(dst, t, cols):
             rows = slice(t * P, (t + 1) * P)
             nc.tensor.matmul_mx(
-                out=y_ps[t][:], lhsT=dw[:, rows].bitcast(FP8X4), lhsT_scale=ds[:, rows],
-                rhs=wa_codes[:].bitcast(FP8X4), rhs_scale=wa_scales[:], start=True, stop=True,
+                out=dst, lhsT=dw[t].bitcast(FP8X4), lhsT_scale=ds[:, rows],
+                rhs=wa_codes[:, cols].bitcast(FP8X4), rhs_scale=wa_scales[:, cols], start=True, stop=True,
             )
-            nc.scalar.copy(win[t][:, :H], y_ps[t][:])
-            nc.scalar.copy(plain[t][:], y_ps[t][:])
-            nc.vector.tensor_tensor(st[t][:], win[t][:].indirect(n1_sb[:]), plain[t][:], ALU.add)
-        for t in range(PACK):
-            nc.scalar.activation(th[t][:], st[t][:], ACT.Tanh)
 
-        gated = [keep.tile([P, HALF], F32, name=f"gated{b}") for b in range(2)]
+        lo_cols, hi_cols = slice(0, HALF), slice(HALF, H)
+        first = (bank[0][:, :HALF], bank[4][:, :HALF])
+        y_product(first[0], 0, lo_cols)
+        y_product(first[1], 0, hi_cols)
+        nc.scalar.activation(win[0][:, lo_cols], first[0], ACT.Copy, scale=gt_sb[:, 0:1])
+        nc.scalar.activation(y_plain[0][:, lo_cols], first[0], ACT.Copy, scale=gt_sb[:, 0:1])
+        nc.scalar.activation(win[0][:, hi_cols], first[1], ACT.Copy, scale=gt_sb[:, 0:1])
+        nc.scalar.activation(y_plain[0][:, hi_cols], first[1], ACT.Copy, scale=gt_sb[:, 0:1])
+        for a, cols in enumerate((lo_cols, hi_cols)):
+            nc.vector.tensor_tensor(
+                st[0][:, cols], win[0][:].indirect(n1_sb[:, a * 16 : (a + 1) * 16]), y_plain[0][:, cols], ALU.add
+            )
+        for t in range(1, PACK):
+            y_product(bank[t][:], t, slice(0, H))
+            nc.scalar.activation(win[t][:, :H], bank[t][:], ACT.Copy, scale=gt_sb[:, t : t + 1])
+            nc.scalar.activation(y_plain[t][:], bank[t][:], ACT.Copy, scale=gt_sb[:, t : t + 1])
+            nc.vector.tensor_tensor(st[t][:], win[t][:].indirect(n1_sb[:]), y_plain[t][:], ALU.add)
+        for t in range(PACK):
+            nc.scalar.activation(th[t][:], st[t][:], ACT.Tanh, scale=gt_inv[:, t : t + 1])
+
+        w1_bf = keep.tile([P, PACK, P, PACK], BF16, name="w1_bf", tag="late", align_bytes=64)
+        w1_dst = w1_bf[:].rearrange("p t m j -> p m t j")
+        w1_src = w1_raw[:].rearrange("p j (m t) -> p m t j", t=PACK)
+        for q in range(4):
+            nc.scalar.copy(w1_dst[:, 32 * q : 32 * q + 32], w1_src[:, 32 * q : 32 * q + 32])
+
         z4 = [keep.tile([P, PACK, HALF], F32, name=f"z4_{a}") for a in range(2)]
         for a in range(2):
             cols = slice(a * HALF, (a + 1) * HALF)
             for t in range(PACK):
-                g = gated[t % 2]
-                nc.scalar.activation(g[:], st[t][:, cols], ACT.Copy, scale=gt_sb[:, t : t + 1])
                 nc.vector.tensor_tensor(
-                    z4[a][:, t, :], th[t][:].indirect(n2_sb[:, a * 16 : (a + 1) * 16]), g[:], ALU.mult
+                    z4[a][:, t, :], th[t][:].indirect(n2_sb[:, a * 16 : (a + 1) * 16]), st[t][:, cols], ALU.mult
                 )
 
-        w1_bf = keep.tile([P, PACK, P, PACK], BF16, name="w1_bf", align_bytes=64)
-        w1_src = w1_raw[:].rearrange("p j (m t) -> p m t j", t=PACK)
-        w1_dst = w1_bf[:].rearrange("p t m j -> p m t j")
-        for q in range(4):
-            nc.scalar.copy(w1_dst[:, 32 * q : 32 * q + 32], w1_src[:, 32 * q : 32 * q + 32])
-        w1_codes = keep.tile([P, N], U32, name="w1_codes", align_bytes=64)
+        w1_codes0 = keep.tile([P, P], U32, name="w1_codes0", align_bytes=64)
         w1_scales = keep.tile([P, N], U8, name="w1_scales", align_bytes=64)
-        nc.vector.quantize_mx(
-            out=w1_codes[:].bitcast(FP8X4), scales=w1_scales[:], in_=w1_bf[:].rearrange("p t m j -> p (t m j)")
-        )
+        w1_cols = w1_bf[:].rearrange("p t m j -> p (t m) j")
+        quantize(w1_codes0[:], w1_scales[:, :P], w1_cols[:, :P, :])
 
-        h_ps = [psum.tile([P, H], F32, name=f"h_ps{t}") for t in range(PACK)]
-        for a in range(2):
-            cols = slice(a * HALF, (a + 1) * HALF)
-            z_bf = keep.tile([P, HALF, PACK], BF16, name=f"z_bf{a}", align_bytes=64)
-            if a == 0:
-                interleave(nc.scalar.copy, z_bf[:], z4[a][:])
-            else:
-                interleave(nc.vector.tensor_copy, z_bf[:, :160, :], z4[a][:, :, :160])
-                interleave(nc.scalar.copy, z_bf[:, 160:, :], z4[a][:, :, 160:])
-            z_codes = keep.tile([P, HALF], U32, name=f"z_codes{a}", align_bytes=64)
-            z_scales = keep.tile([P, HALF], U8, name=f"z_scales{a}", align_bytes=64)
-            nc.vector.quantize_mx(
-                out=z_codes[:].bitcast(FP8X4), scales=z_scales[:], in_=z_bf[:].rearrange("p c j -> p (c j)")
+        z_bf = [keep.tile([P, HALF, PACK], BF16, name=f"z_bf{a}", tag=f"z_bf{a}", align_bytes=64) for a in range(2)]
+        z_codes = keep.tile([P, H], U32, name="z_codes", align_bytes=64)
+        z_scales = keep.tile([P, H], U8, name="z_scales", align_bytes=64)
+        interleave(nc.scalar.copy, z_bf[0][:], z4[0][:])
+        interleave(nc.vector.tensor_copy, z_bf[1][:, :192, :], z4[1][:, :, :192])
+        interleave(nc.scalar.copy, z_bf[1][:, 192:, :], z4[1][:, :, 192:])
+
+        def h_product(dst, codes, t, cols):
+            rows = slice(t * P, (t + 1) * P)
+            nc.tensor.matmul_mx(
+                out=dst, lhsT=codes.bitcast(FP8X4), lhsT_scale=w1_scales[:, rows],
+                rhs=z_codes[:, cols].bitcast(FP8X4), rhs_scale=z_scales[:, cols], start=True, stop=True,
             )
-            for t in range(PACK):
-                rows = slice(t * P, (t + 1) * P)
-                nc.tensor.matmul_mx(
-                    out=h_ps[t][:, cols], lhsT=w1_codes[:, rows].bitcast(FP8X4), lhsT_scale=w1_scales[:, rows],
-                    rhs=z_codes[:].bitcast(FP8X4), rhs_scale=z_scales[:], start=True, stop=True,
-                )
-                nc.scalar.copy(win[t][:, cols], h_ps[t][:, cols])
-                nc.scalar.copy(plain[t][:, cols], h_ps[t][:, cols])
+
+        for a, cols in enumerate((lo_cols, hi_cols)):
+            quantize(z_codes[:, cols], z_scales[:, cols], z_bf[a][:])
+            h_product(bank[a][:, :HALF], w1_codes0[:], 0, cols)
+        w1_codes_rest = keep.tile([P, N - P], U32, name="w1_codes_rest", tag="z_bf1", align_bytes=64)
+        quantize(w1_codes_rest[:, :P], w1_scales[:, P:HALF], w1_cols[:, P:HALF, :])
+        quantize(w1_codes_rest[:, P:], w1_scales[:, HALF:], w1_cols[:, HALF:, :])
+        nc.scalar.activation(win[0][:, lo_cols], bank[0][:, :HALF], ACT.Copy, scale=0.5)
+        nc.scalar.activation(plain[0][:, lo_cols], bank[0][:, :HALF], ACT.Copy, scale=0.5)
+        nc.vector.tensor_scalar(win[0][:, hi_cols], bank[1][:, :HALF], 0.5, None, ALU.mult)
+        nc.scalar.activation(plain[0][:, hi_cols], bank[1][:, :HALF], ACT.Copy, scale=0.5)
+        for t in range(1, PACK):
+            h_product(bank[4 + t][:], w1_codes_rest[:, (t - 1) * P : t * P], t, slice(0, H))
+            nc.scalar.activation(win[t][:, :H], bank[4 + t][:], ACT.Copy, scale=0.5)
+            nc.scalar.activation(plain[t][:], bank[4 + t][:], ACT.Copy, scale=0.5)
 
         out_rows = out.rearrange("(p t) j -> p t j", t=PACK)
-        for t in range(PACK):
-            d1, d2 = st[t], th[t]
-            hi = keep.tile([P, H], F32, name=f"hi{t}")
-            lo = keep.tile([P, H], F32, name=f"lo{t}")
-            mid = keep.tile([P, H], F32, name=f"mid{t}")
-            res = keep.tile([P, H], F32, name=f"res{t}")
-            nc.vector.tensor_tensor(d1[:], win[t][:].indirect(n3_sb[:]), plain[t][:], ALU.subtract)
-            nc.vector.tensor_tensor(d2[:], win[t][:].indirect(n4_sb[:]), plain[t][:], ALU.subtract)
-            nc.vector.scalar_tensor_tensor(hi[:], d1[:], 0.0, d2[:], ALU.max, ALU.max)
-            nc.vector.scalar_tensor_tensor(lo[:], d1[:], 0.0, d2[:], ALU.min, ALU.min)
-            nc.vector.scalar_tensor_tensor(mid[:], h_ps[t][:], 0.5, hi[:], ALU.mult, ALU.add)
-            nc.vector.scalar_tensor_tensor(res[:], lo[:], -0.5, mid[:], ALU.mult, ALU.add)
-            nc.sync.dma_start(out_rows[:, t, :], res[:])
+        hi = [keep.tile([P, H], F32, name=f"hi{t}") for t in range(PACK)]
+        lo = [keep.tile([P, H], F32, name=f"lo{t}") for t in range(PACK)]
+        res = [keep.tile([P, H], F32, name=f"res{t}") for t in range(PACK)]
+
+        e1 = [st[(2 * t) % 3] for t in range(PACK)]
+        e2 = [st[(2 * t + 1) % 3] for t in range(PACK)]
+
+        def diff(dst, t, lst, c0, c1):
+            nc.vector.tensor_tensor(
+                dst[:, c0:c1], win[t][:].indirect(lst[:, c0 // 16 : c1 // 16]), plain[t][:, c0:c1], ALU.subtract
+            )
+
+        def extreme(dst, t, op, c0, c1):
+            nc.vector.scalar_tensor_tensor(dst[:, c0:c1], e1[t][:, c0:c1], 0.0, e2[t][:, c0:c1], op, op)
+
+        neg = keep.tile([P, H], F32, name="neg")
+
+        def sum_on_tensor(t):
+            turned = keep.tile([P, H], F32, name=f"turned{t}")
+            nc.scalar.activation(neg[:], lo[t][:], ACT.Copy, scale=-1.0)
+            fwd = [bank[b][:, :P] for b in (2, 3, 4, 0)]
+            for q in range(4):
+                blk = slice(q * P, (q + 1) * P)
+                for i, term in enumerate((plain[t], hi[t], hi[t])):
+                    nc.tensor.matmul(fwd[q], term[:, blk], ident[:], start=(i == 0), stop=False, is_transpose=True)
+            for q in range(4):
+                blk = slice(q * P, (q + 1) * P)
+                nc.tensor.matmul(fwd[q], neg[:, blk], ident[:], start=False, stop=True, is_transpose=True)
+                nc.scalar.copy(turned[:, blk], fwd[q])
+            for a in range(2):
+                cols = slice(a * HALF, (a + 1) * HALF)
+                back = bank[1 + 4 * a]
+                for q in range(2):
+                    src = slice(a * HALF + q * P, a * HALF + (q + 1) * P)
+                    nc.tensor.transpose(back[:, q * P : (q + 1) * P], turned[:, src], ident[:])
+                nc.scalar.copy(res[t][:, cols], back[:, :HALF])
+            nc.sync.dma_start(out_rows[:, t, :], res[t][:])
+
+        diff(e1[0], 0, n3_sb, 0, HALF)
+        diff(e1[0], 0, n3_sb, HALF, H)
+        for t in range(PACK - 1):
+            diff(e2[t], t, n4_sb, 0, H)
+            diff(e1[t + 1], t + 1, n3_sb, 0, H)
+            extreme(hi[t], t, ALU.max, 0, H)
+            extreme(lo[t], t, ALU.min, 0, H)
+            sum_on_tensor(t)
+        t = PACK - 1
+        mid = keep.tile([P, H], F32, name="mid")
+        for a in range(2):
+            diff(e2[t], t, n4_sb, a * HALF, (a + 1) * HALF)
+        for a in range(2):
+            extreme(hi[t], t, ALU.max, a * HALF, (a + 1) * HALF)
+            extreme(lo[t], t, ALU.min, a * HALF, (a + 1) * HALF)
+        for a in range(2):
+            cols = slice(a * HALF, (a + 1) * HALF)
+            nc.vector.scalar_tensor_tensor(mid[:, cols], hi[t][:, cols], 2.0, plain[t][:, cols], ALU.mult, ALU.add)
+        for a in range(2):
+            cols = slice(a * HALF, (a + 1) * HALF)
+            nc.vector.tensor_tensor(res[t][:, cols], mid[:, cols], lo[t][:, cols], ALU.subtract)
+            nc.sync.dma_start(out_rows[:, t, cols], res[t][:, cols])

@@ -18,7 +18,15 @@ ACT = mybir.ActivationFunctionType
 
 P = 128
 PACK = 4
-HALF = 256
+LIST_ROWS = 16
+HALF = H // 2
+LEFT, RIGHT, WHOLE = slice(0, HALF), slice(HALF, H), slice(0, H)
+LAST = PACK - 1
+FINITE = 3.0e38
+WA_VECTOR_COLS = 128
+Z_VECTOR_COLS = 192
+W1_PIECES = 4
+RING = 3
 
 
 def tile_picked_tokhopprange_none_p_kernel(
@@ -29,27 +37,43 @@ def tile_picked_tokhopprange_none_p_kernel(
         keep = ctx.enter_context(tc.tile_pool(name="keep", bufs=1))
         psum = ctx.enter_context(tc.psum_pool(name="psum", bufs=1))
 
-        def list_tile(name):
-            return keep.tile([P, S // 16], U16, name=name)
+        def entries(list_sb, cols):
+            return list_sb[:, cols.start // LIST_ROWS : cols.stop // LIST_ROWS]
 
-        offs_sb, n1_sb, n2_sb, n3_sb, n4_sb = [list_tile(nm) for nm in ("offs_sb", "n1_sb", "n2_sb", "n3_sb", "n4_sb")]
+        def round_and_interleave(copy, dst, src):
+            copy(dst.rearrange("p (c i) t -> p c t i", i=4), src.rearrange("p t (c i) -> p c t i", i=4))
 
-        xs = keep.tile([P, T], U8, name="xs", tag="xs", align_bytes=64)
-        xw = keep.tile([P, T], U32, name="xw", align_bytes=64)
-        nc.gpsimd.memset(xs[:].bitcast(I32), 0)
-        warm_in = keep.tile([P, 1], F32, name="warm_in")
-        warm_out = keep.tile([P, 1], F32, name="warm_out")
-        nc.vector.memset(warm_in[:], 0.0)
-        nc.scalar.activation(warm_out[:], warm_in[:], ACT.Tanh)
+        def round_shared(dst, src, vector_cols):
+            round_and_interleave(nc.vector.tensor_copy, dst[:, :vector_cols, :], src[:, :, :vector_cols])
+            round_and_interleave(nc.scalar.copy, dst[:, vector_cols:, :], src[:, :, vector_cols:])
+
+        def quantize(codes, scales, rounded):
+            nc.vector.quantize_mx(out=codes.bitcast(FP8X4), scales=scales, in_=rounded.rearrange("p c t -> p (c t)"))
+
+        def product(dst, lhs_codes, lhs_scales, rhs_codes, rhs_scales):
+            nc.tensor.matmul_mx(
+                out=dst, lhsT=lhs_codes.bitcast(FP8X4), lhsT_scale=lhs_scales,
+                rhs=rhs_codes.bitcast(FP8X4), rhs_scale=rhs_scales, start=True, stop=True,
+            )
+
+        def scaled_copy(dst, src, scale):
+            nc.scalar.activation(dst, src, ACT.Copy, scale=scale)
+
+        offs_sb, n1_sb, n2_sb, n3_sb, n4_sb = [
+            keep.tile([P, S // LIST_ROWS], U16, name=name) for name in ("offs_sb", "n1_sb", "n2_sb", "n3_sb", "n4_sb")
+        ]
+        x_scales_sb = keep.tile([P, T], U8, name="x_scales_sb", tag="x_scales_sb", align_bytes=64)
+        x_words_sb = keep.tile([P, T], U32, name="x_words_sb", align_bytes=64)
+        nc.gpsimd.memset(x_scales_sb[:].bitcast(I32), 0)
 
         nc.sync.dma_start(offs_sb[:], offs)
         wa_rows = wa.rearrange("(p j) c -> p j c", j=PACK)
         wa_raw = [keep.tile([P, PACK, HALF], F32, name=f"wa_raw{a}", tag=f"wa_raw{a}") for a in range(2)]
-        nc.sync.dma_start(wa_raw[0][:], wa_rows[:, :, :HALF])
-        for q in range(4):
-            nc.sync.dma_start(xs[q:P:32, :].bitcast(I32), x_scales[0, q:16:4, :].bitcast(I32))
-        nc.sync.dma_start(xw[:].bitcast(I32), x_words[0].rearrange("p c r -> p (c r)").bitcast(I32))
-        nc.sync.dma_start(wa_raw[1][:], wa_rows[:, :, HALF:])
+        nc.sync.dma_start(wa_raw[0][:], wa_rows[:, :, LEFT])
+        for r in range(4):
+            nc.sync.dma_start(x_scales_sb[r:P:32, :].bitcast(I32), x_scales[0, r:16:4, :].bitcast(I32))
+        nc.sync.dma_start(x_words_sb[:].bitcast(I32), x_words[0].rearrange("p c r -> p (c r)").bitcast(I32))
+        nc.sync.dma_start(wa_raw[1][:], wa_rows[:, :, RIGHT])
         gt_sb = keep.tile([P, PACK], F32, name="gt_sb")
         nc.sync.dma_start(gt_sb[:], gt.rearrange("(p t) o -> p (t o)", t=PACK))
         nc.sync.dma_start(n1_sb[:], n1)
@@ -59,97 +83,84 @@ def tile_picked_tokhopprange_none_p_kernel(
         nc.sync.dma_start(n3_sb[:], n3)
         nc.sync.dma_start(n4_sb[:], n4)
 
-        win = [keep.tile([P, 2 * H], F32, name=f"win{t}") for t in range(PACK)]
+        window = [keep.tile([P, 2 * H], F32, name=f"window{t}") for t in range(PACK)]
         for t in range(PACK):
-            nc.gpsimd.memset(win[t][:, H:], 0.0)
-
+            nc.vector.memset(window[t][:, H:], 0.0)
         ident = keep.tile([P, P], F32, name="ident")
         make_identity(nc, ident[:])
 
-        gs = keep.tile([P, S], U8, name="gs", align_bytes=64)
-        gw = keep.tile([P, S], U32, name="gw", align_bytes=64)
-        ds = keep.tile([P, S], U8, name="ds", align_bytes=64)
-        dw0 = keep.tile([P, P], U32, name="dw0", align_bytes=64)
-
-        def interleave(engine_copy, dst, src):
-            engine_copy(
-                dst.rearrange("p (c i) t -> p c t i", i=4),
-                src.rearrange("p t (c i) -> p c t i", i=4),
-            )
-
+        picked_scales = keep.tile([P, S], U8, name="picked_scales", align_bytes=64)
+        picked_words = keep.tile([P, S], U32, name="picked_words", align_bytes=64)
+        token_scales = keep.tile([P, S], U8, name="token_scales", align_bytes=64)
+        token_words0 = keep.tile([P, P], U32, name="token_words0", align_bytes=64)
         wa_scales = keep.tile([P, H], U8, name="wa_scales", align_bytes=64)
         wa_bf = [keep.tile([P, HALF, PACK], BF16, name=f"wa_bf{a}", tag=f"wa_bf{a}", align_bytes=64) for a in range(2)]
 
-        def quantize(codes, scales, bf):
-            nc.vector.quantize_mx(out=codes.bitcast(FP8X4), scales=scales, in_=bf.rearrange("p c j -> p (c j)"))
-
-        interleave(nc.scalar.copy, wa_bf[0][:], wa_raw[0][:])
-        nc.vector.tensor_copy(gs[:], xs[:].indirect(offs_sb[:]))
-        wa_codes = keep.tile([P, H], U32, name="wa_codes", tag="xs", align_bytes=64)
-        quantize(wa_codes[:, :HALF], wa_scales[:, :HALF], wa_bf[0][:])
-        nc.vector.tensor_copy(ds[:].rearrange("p (t m) -> p t m", t=PACK), gs[:].rearrange("p (m t) -> p t m", t=PACK))
-        nc.vector.tensor_copy(gw[:], xw[:].indirect(offs_sb[:]))
-        gw_by_tile = gw[:].bitcast(I32).rearrange("p (m t) -> p t m", t=PACK)
-        nc.vector.tensor_copy(dw0[:].bitcast(I32), gw_by_tile[:, 0, :])
-        interleave(nc.vector.tensor_copy, wa_bf[1][:, :P, :], wa_raw[1][:, :, :P])
-        interleave(nc.scalar.copy, wa_bf[1][:, P:, :], wa_raw[1][:, :, P:])
-        quantize(wa_codes[:, HALF:], wa_scales[:, HALF:], wa_bf[1][:])
-        dw_rest = keep.tile([P, PACK - 1, P], U32, name="dw_rest", tag="wa_bf1", align_bytes=64)
-        nc.vector.tensor_copy(dw_rest[:].bitcast(I32), gw_by_tile[:, 1:, :])
-        dw = [dw0[:]] + [dw_rest[:, t, :] for t in range(PACK - 1)]
+        round_and_interleave(nc.scalar.copy, wa_bf[0][:], wa_raw[0][:])
+        nc.vector.tensor_copy(picked_scales[:], x_scales_sb[:].indirect(offs_sb[:]))
+        wa_codes = keep.tile([P, H], U32, name="wa_codes", tag="x_scales_sb", align_bytes=64)
+        quantize(wa_codes[:, LEFT], wa_scales[:, LEFT], wa_bf[0][:])
+        nc.vector.tensor_copy(
+            token_scales[:].rearrange("p (t m) -> p t m", t=PACK), picked_scales[:].rearrange("p (m t) -> p t m", t=PACK)
+        )
+        nc.vector.tensor_copy(picked_words[:], x_words_sb[:].indirect(offs_sb[:]))
+        picked_by_tile = picked_words[:].bitcast(I32).rearrange("p (m t) -> p t m", t=PACK)
+        nc.vector.tensor_copy(token_words0[:].bitcast(I32), picked_by_tile[:, 0, :])
+        round_shared(wa_bf[1][:], wa_raw[1][:], WA_VECTOR_COLS)
+        quantize(wa_codes[:, RIGHT], wa_scales[:, RIGHT], wa_bf[1][:])
+        token_words_rest = keep.tile([P, LAST, P], U32, name="token_words_rest", tag="wa_bf1", align_bytes=64)
+        nc.vector.tensor_copy(token_words_rest[:].bitcast(I32), picked_by_tile[:, 1:, :])
+        token_words = [token_words0[:]] + [token_words_rest[:, t, :] for t in range(LAST)]
 
         gt_safe = keep.tile([P, PACK], F32, name="gt_safe", tag="wa_raw1")
-        gt_rec = keep.tile([P, PACK], F32, name="gt_rec")
-        gt_inv = keep.tile([P, PACK], F32, name="gt_inv")
+        gt_reciprocal = keep.tile([P, PACK], F32, name="gt_reciprocal")
+        gt_inverse = keep.tile([P, PACK], F32, name="gt_inverse")
         nc.vector.scalar_tensor_tensor(gt_safe[:], gt_sb[:], 0.0, gt_sb[:], ALU.is_equal, ALU.add)
-        nc.vector.reciprocal(gt_rec[:], gt_safe[:])
-        nc.vector.tensor_scalar(gt_inv[:], gt_rec[:], 3.0e38, -3.0e38, ALU.min, ALU.max)
+        nc.vector.reciprocal(gt_reciprocal[:], gt_safe[:])
+        nc.vector.tensor_scalar(gt_inverse[:], gt_reciprocal[:], FINITE, -FINITE, ALU.min, ALU.max)
 
         bank = [psum.tile([P, H], F32, name=f"bank{b}") for b in range(8)]
-        plain = [keep.tile([P, H], F32, name=f"plain{t}") for t in range(PACK)]
-        y_plain = plain[: PACK - 1] + [keep.tile([P, H], F32, name="y_plain3", tag="late", align_bytes=64)]
-        st = [keep.tile([P, H], F32, name=f"st{t}") for t in range(PACK)]
-        th = [keep.tile([P, H], F32, name=f"th{t}") for t in range(PACK)]
+        twin = [keep.tile([P, H], F32, name=f"twin{t}") for t in range(PACK)]
+        y_twin = twin[:LAST] + [keep.tile([P, H], F32, name="y_twin_last", tag="y_twin_last", align_bytes=64)]
+        gated_st = [keep.tile([P, H], F32, name=f"gated_st{t}") for t in range(PACK)]
+        tanh_st = [keep.tile([P, H], F32, name=f"tanh_st{t}") for t in range(PACK)]
 
         def y_product(dst, t, cols):
-            rows = slice(t * P, (t + 1) * P)
-            nc.tensor.matmul_mx(
-                out=dst, lhsT=dw[t].bitcast(FP8X4), lhsT_scale=ds[:, rows],
-                rhs=wa_codes[:, cols].bitcast(FP8X4), rhs_scale=wa_scales[:, cols], start=True, stop=True,
-            )
+            product(dst, token_words[t], token_scales[:, t * P : (t + 1) * P], wa_codes[:, cols], wa_scales[:, cols])
 
-        lo_cols, hi_cols = slice(0, HALF), slice(HALF, H)
-        first = (bank[0][:, :HALF], bank[4][:, :HALF])
-        y_product(first[0], 0, lo_cols)
-        y_product(first[1], 0, hi_cols)
-        nc.scalar.activation(win[0][:, lo_cols], first[0], ACT.Copy, scale=gt_sb[:, 0:1])
-        nc.scalar.activation(y_plain[0][:, lo_cols], first[0], ACT.Copy, scale=gt_sb[:, 0:1])
-        nc.scalar.activation(win[0][:, hi_cols], first[1], ACT.Copy, scale=gt_sb[:, 0:1])
-        nc.scalar.activation(y_plain[0][:, hi_cols], first[1], ACT.Copy, scale=gt_sb[:, 0:1])
-        for a, cols in enumerate((lo_cols, hi_cols)):
+        def add_looked_up_y(t, cols):
             nc.vector.tensor_tensor(
-                st[0][:, cols], win[0][:].indirect(n1_sb[:, a * 16 : (a + 1) * 16]), y_plain[0][:, cols], ALU.add
+                gated_st[t][:, cols], window[t][:].indirect(entries(n1_sb, cols)), y_twin[t][:, cols], ALU.add
             )
-        for t in range(1, PACK):
-            y_product(bank[t][:], t, slice(0, H))
-            nc.scalar.activation(win[t][:, :H], bank[t][:], ACT.Copy, scale=gt_sb[:, t : t + 1])
-            nc.scalar.activation(y_plain[t][:], bank[t][:], ACT.Copy, scale=gt_sb[:, t : t + 1])
-            nc.vector.tensor_tensor(st[t][:], win[t][:].indirect(n1_sb[:]), y_plain[t][:], ALU.add)
-        for t in range(PACK):
-            nc.scalar.activation(th[t][:], st[t][:], ACT.Tanh, scale=gt_inv[:, t : t + 1])
 
-        w1_bf = keep.tile([P, PACK, P, PACK], BF16, name="w1_bf", tag="late", align_bytes=64)
+        y_halves = ((LEFT, bank[0][:, :HALF]), (RIGHT, bank[4][:, :HALF]))
+        for cols, y_half in y_halves:
+            y_product(y_half, 0, cols)
+        for cols, y_half in y_halves:
+            scaled_copy(window[0][:, cols], y_half, gt_sb[:, 0:1])
+            scaled_copy(y_twin[0][:, cols], y_half, gt_sb[:, 0:1])
+        for cols in (LEFT, RIGHT):
+            add_looked_up_y(0, cols)
+        for t in range(1, PACK):
+            y_product(bank[t][:], t, WHOLE)
+            scaled_copy(window[t][:, WHOLE], bank[t][:], gt_sb[:, t : t + 1])
+            scaled_copy(y_twin[t][:], bank[t][:], gt_sb[:, t : t + 1])
+            add_looked_up_y(t, WHOLE)
+        for t in range(PACK):
+            nc.scalar.activation(tanh_st[t][:], gated_st[t][:], ACT.Tanh, scale=gt_inverse[:, t : t + 1])
+
+        w1_bf = keep.tile([P, PACK, P, PACK], BF16, name="w1_bf", tag="y_twin_last", align_bytes=64)
         w1_dst = w1_bf[:].rearrange("p t m j -> p m t j")
         w1_src = w1_raw[:].rearrange("p j (m t) -> p m t j", t=PACK)
-        for q in range(4):
-            nc.scalar.copy(w1_dst[:, 32 * q : 32 * q + 32], w1_src[:, 32 * q : 32 * q + 32])
+        piece = P // W1_PIECES
+        for q in range(W1_PIECES):
+            nc.scalar.copy(w1_dst[:, q * piece : (q + 1) * piece], w1_src[:, q * piece : (q + 1) * piece])
 
-        z4 = [keep.tile([P, PACK, HALF], F32, name=f"z4_{a}") for a in range(2)]
-        for a in range(2):
-            cols = slice(a * HALF, (a + 1) * HALF)
+        z = [keep.tile([P, PACK, HALF], F32, name=f"z{a}") for a in range(2)]
+        for a, cols in enumerate((LEFT, RIGHT)):
             for t in range(PACK):
                 nc.vector.tensor_tensor(
-                    z4[a][:, t, :], th[t][:].indirect(n2_sb[:, a * 16 : (a + 1) * 16]), st[t][:, cols], ALU.mult
+                    z[a][:, t, :], tanh_st[t][:].indirect(entries(n2_sb, cols)), gated_st[t][:, cols], ALU.mult
                 )
 
         w1_codes0 = keep.tile([P, P], U32, name="w1_codes0", align_bytes=64)
@@ -160,90 +171,79 @@ def tile_picked_tokhopprange_none_p_kernel(
         z_bf = [keep.tile([P, HALF, PACK], BF16, name=f"z_bf{a}", tag=f"z_bf{a}", align_bytes=64) for a in range(2)]
         z_codes = keep.tile([P, H], U32, name="z_codes", align_bytes=64)
         z_scales = keep.tile([P, H], U8, name="z_scales", align_bytes=64)
-        interleave(nc.scalar.copy, z_bf[0][:], z4[0][:])
-        interleave(nc.vector.tensor_copy, z_bf[1][:, :192, :], z4[1][:, :, :192])
-        interleave(nc.scalar.copy, z_bf[1][:, 192:, :], z4[1][:, :, 192:])
+        round_and_interleave(nc.scalar.copy, z_bf[0][:], z[0][:])
+        round_shared(z_bf[1][:], z[1][:], Z_VECTOR_COLS)
 
         def h_product(dst, codes, t, cols):
-            rows = slice(t * P, (t + 1) * P)
-            nc.tensor.matmul_mx(
-                out=dst, lhsT=codes.bitcast(FP8X4), lhsT_scale=w1_scales[:, rows],
-                rhs=z_codes[:, cols].bitcast(FP8X4), rhs_scale=z_scales[:, cols], start=True, stop=True,
-            )
+            product(dst, codes, w1_scales[:, t * P : (t + 1) * P], z_codes[:, cols], z_scales[:, cols])
 
-        for a, cols in enumerate((lo_cols, hi_cols)):
+        for a, cols in enumerate((LEFT, RIGHT)):
             quantize(z_codes[:, cols], z_scales[:, cols], z_bf[a][:])
             h_product(bank[a][:, :HALF], w1_codes0[:], 0, cols)
         w1_codes_rest = keep.tile([P, N - P], U32, name="w1_codes_rest", tag="z_bf1", align_bytes=64)
-        quantize(w1_codes_rest[:, :P], w1_scales[:, P:HALF], w1_cols[:, P:HALF, :])
-        quantize(w1_codes_rest[:, P:], w1_scales[:, HALF:], w1_cols[:, HALF:, :])
-        nc.scalar.activation(win[0][:, lo_cols], bank[0][:, :HALF], ACT.Copy, scale=0.5)
-        nc.scalar.activation(plain[0][:, lo_cols], bank[0][:, :HALF], ACT.Copy, scale=0.5)
-        nc.vector.tensor_scalar(win[0][:, hi_cols], bank[1][:, :HALF], 0.5, None, ALU.mult)
-        nc.scalar.activation(plain[0][:, hi_cols], bank[1][:, :HALF], ACT.Copy, scale=0.5)
+        quantize(w1_codes_rest[:, :P], w1_scales[:, P : 2 * P], w1_cols[:, P : 2 * P, :])
+        quantize(w1_codes_rest[:, P:], w1_scales[:, 2 * P :], w1_cols[:, 2 * P :, :])
+        scaled_copy(window[0][:, LEFT], bank[0][:, :HALF], 0.5)
+        scaled_copy(twin[0][:, LEFT], bank[0][:, :HALF], 0.5)
+        nc.vector.tensor_scalar(window[0][:, RIGHT], bank[1][:, :HALF], 0.5, None, ALU.mult)
+        scaled_copy(twin[0][:, RIGHT], bank[1][:, :HALF], 0.5)
         for t in range(1, PACK):
-            h_product(bank[4 + t][:], w1_codes_rest[:, (t - 1) * P : t * P], t, slice(0, H))
-            nc.scalar.activation(win[t][:, :H], bank[4 + t][:], ACT.Copy, scale=0.5)
-            nc.scalar.activation(plain[t][:], bank[4 + t][:], ACT.Copy, scale=0.5)
+            h_product(bank[4 + t][:], w1_codes_rest[:, (t - 1) * P : t * P], t, WHOLE)
+            scaled_copy(window[t][:, WHOLE], bank[4 + t][:], 0.5)
+            scaled_copy(twin[t][:], bank[4 + t][:], 0.5)
 
         out_rows = out.rearrange("(p t) j -> p t j", t=PACK)
-        hi = [keep.tile([P, H], F32, name=f"hi{t}") for t in range(PACK)]
-        lo = [keep.tile([P, H], F32, name=f"lo{t}") for t in range(PACK)]
-        res = [keep.tile([P, H], F32, name=f"res{t}") for t in range(PACK)]
+        above = [keep.tile([P, H], F32, name=f"above{t}") for t in range(PACK)]
+        below = [keep.tile([P, H], F32, name=f"below{t}") for t in range(PACK)]
+        result = [keep.tile([P, H], F32, name=f"result{t}") for t in range(PACK)]
+        da = [gated_st[(2 * t) % RING] for t in range(PACK)]
+        db = [gated_st[(2 * t + 1) % RING] for t in range(PACK)]
+        minus_below = keep.tile([P, H], F32, name="minus_below")
 
-        e1 = [st[(2 * t) % 3] for t in range(PACK)]
-        e2 = [st[(2 * t + 1) % 3] for t in range(PACK)]
-
-        def diff(dst, t, lst, c0, c1):
+        def difference(dst, t, list_sb, cols):
             nc.vector.tensor_tensor(
-                dst[:, c0:c1], win[t][:].indirect(lst[:, c0 // 16 : c1 // 16]), plain[t][:, c0:c1], ALU.subtract
+                dst[:, cols], window[t][:].indirect(entries(list_sb, cols)), twin[t][:, cols], ALU.subtract
             )
 
-        def extreme(dst, t, op, c0, c1):
-            nc.vector.scalar_tensor_tensor(dst[:, c0:c1], e1[t][:, c0:c1], 0.0, e2[t][:, c0:c1], op, op)
+        def extreme(dst, t, op, cols):
+            nc.vector.scalar_tensor_tensor(dst[:, cols], da[t][:, cols], 0.0, db[t][:, cols], op, op)
 
-        neg = keep.tile([P, H], F32, name="neg")
-
-        def sum_on_tensor(t):
+        def sum_on_tensor_engine(t):
             turned = keep.tile([P, H], F32, name=f"turned{t}")
-            nc.scalar.activation(neg[:], lo[t][:], ACT.Copy, scale=-1.0)
-            fwd = [bank[b][:, :P] for b in (2, 3, 4, 0)]
-            for q in range(4):
-                blk = slice(q * P, (q + 1) * P)
-                for i, term in enumerate((plain[t], hi[t], hi[t])):
-                    nc.tensor.matmul(fwd[q], term[:, blk], ident[:], start=(i == 0), stop=False, is_transpose=True)
-            for q in range(4):
-                blk = slice(q * P, (q + 1) * P)
-                nc.tensor.matmul(fwd[q], neg[:, blk], ident[:], start=False, stop=True, is_transpose=True)
-                nc.scalar.copy(turned[:, blk], fwd[q])
-            for a in range(2):
-                cols = slice(a * HALF, (a + 1) * HALF)
-                back = bank[1 + 4 * a]
+            scaled_copy(minus_below[:], below[t][:], -1.0)
+            sums = [bank[b][:, :P] for b in (2, 3, 4, 0)]
+            blocks = [slice(q * P, (q + 1) * P) for q in range(H // P)]
+            for block_sum, block in zip(sums, blocks):
+                for i, term in enumerate((twin[t], above[t], above[t])):
+                    nc.tensor.matmul(block_sum, term[:, block], ident[:], start=(i == 0), stop=False, is_transpose=True)
+            for block_sum, block in zip(sums, blocks):
+                nc.tensor.matmul(block_sum, minus_below[:, block], ident[:], start=False, stop=True, is_transpose=True)
+                nc.scalar.copy(turned[:, block], block_sum)
+            for a, (cols, back) in enumerate(((LEFT, bank[1]), (RIGHT, bank[5]))):
                 for q in range(2):
-                    src = slice(a * HALF + q * P, a * HALF + (q + 1) * P)
-                    nc.tensor.transpose(back[:, q * P : (q + 1) * P], turned[:, src], ident[:])
-                nc.scalar.copy(res[t][:, cols], back[:, :HALF])
-            nc.sync.dma_start(out_rows[:, t, :], res[t][:])
+                    nc.tensor.transpose(back[:, blocks[q]], turned[:, blocks[2 * a + q]], ident[:])
+                nc.scalar.copy(result[t][:, cols], back[:, :HALF])
+                nc.sync.dma_start(out_rows[:, t, cols], result[t][:, cols])
 
-        diff(e1[0], 0, n3_sb, 0, HALF)
-        diff(e1[0], 0, n3_sb, HALF, H)
-        for t in range(PACK - 1):
-            diff(e2[t], t, n4_sb, 0, H)
-            diff(e1[t + 1], t + 1, n3_sb, 0, H)
-            extreme(hi[t], t, ALU.max, 0, H)
-            extreme(lo[t], t, ALU.min, 0, H)
-            sum_on_tensor(t)
-        t = PACK - 1
-        mid = keep.tile([P, H], F32, name="mid")
-        for a in range(2):
-            diff(e2[t], t, n4_sb, a * HALF, (a + 1) * HALF)
-        for a in range(2):
-            extreme(hi[t], t, ALU.max, a * HALF, (a + 1) * HALF)
-            extreme(lo[t], t, ALU.min, a * HALF, (a + 1) * HALF)
-        for a in range(2):
-            cols = slice(a * HALF, (a + 1) * HALF)
-            nc.vector.scalar_tensor_tensor(mid[:, cols], hi[t][:, cols], 2.0, plain[t][:, cols], ALU.mult, ALU.add)
-        for a in range(2):
-            cols = slice(a * HALF, (a + 1) * HALF)
-            nc.vector.tensor_tensor(res[t][:, cols], mid[:, cols], lo[t][:, cols], ALU.subtract)
-            nc.sync.dma_start(out_rows[:, t, cols], res[t][:, cols])
+        for cols in (LEFT, RIGHT):
+            difference(da[0], 0, n3_sb, cols)
+        for t in range(LAST):
+            difference(db[t], t, n4_sb, WHOLE)
+            difference(da[t + 1], t + 1, n3_sb, WHOLE)
+            extreme(above[t], t, ALU.max, WHOLE)
+            extreme(below[t], t, ALU.min, WHOLE)
+            sum_on_tensor_engine(t)
+
+        upper = keep.tile([P, H], F32, name="upper")
+        for cols in (LEFT, RIGHT):
+            difference(db[LAST], LAST, n4_sb, cols)
+        for cols in (LEFT, RIGHT):
+            extreme(above[LAST], LAST, ALU.max, cols)
+            extreme(below[LAST], LAST, ALU.min, cols)
+        for cols in (LEFT, RIGHT):
+            nc.vector.scalar_tensor_tensor(
+                upper[:, cols], above[LAST][:, cols], 2.0, twin[LAST][:, cols], ALU.mult, ALU.add
+            )
+        for cols in (LEFT, RIGHT):
+            nc.vector.tensor_tensor(result[LAST][:, cols], upper[:, cols], below[LAST][:, cols], ALU.subtract)
+            nc.sync.dma_start(out_rows[:, LAST, cols], result[LAST][:, cols])

from contextlib import ExitStack

import concourse.mybir as mybir
from concourse.masks import make_identity

K, T, S, N, H = 512, 2048, 512, 512, 512
FLOPS = 2 * K * S * H + 2 * S * N * H

F32 = mybir.dt.float32
BF16 = mybir.dt.bfloat16
I32 = mybir.dt.int32
U32 = mybir.dt.uint32
U16 = mybir.dt.uint16
U8 = mybir.dt.uint8
FP8X4 = mybir.dt.float8_e4m3fn_x4
ALU = mybir.AluOpType
ACT = mybir.ActivationFunctionType

P = 128
PACK = 4
LIST_ROWS = 16
HALF = H // 2
LEFT, RIGHT, WHOLE = slice(0, HALF), slice(HALF, H), slice(0, H)
LAST = PACK - 1
FINITE = 3.0e38
WA_VECTOR_COLS = 128
Z_VECTOR_COLS = 192
W1_PIECES = 4
RING = 3


def tile_picked_tokhopprange_none_p_kernel(
    tc, x_words, x_scales, wa, gt, w1, offs, n1, n2, n3, n4, out
):
    nc = tc.nc
    with ExitStack() as ctx:
        keep = ctx.enter_context(tc.tile_pool(name="keep", bufs=1))
        psum = ctx.enter_context(tc.psum_pool(name="psum", bufs=1))

        def entries(list_sb, cols):
            return list_sb[:, cols.start // LIST_ROWS : cols.stop // LIST_ROWS]

        def round_and_interleave(copy, dst, src):
            copy(dst.rearrange("p (c i) t -> p c t i", i=4), src.rearrange("p t (c i) -> p c t i", i=4))

        def round_shared(dst, src, vector_cols):
            round_and_interleave(nc.vector.tensor_copy, dst[:, :vector_cols, :], src[:, :, :vector_cols])
            round_and_interleave(nc.scalar.copy, dst[:, vector_cols:, :], src[:, :, vector_cols:])

        def quantize(codes, scales, rounded):
            nc.vector.quantize_mx(out=codes.bitcast(FP8X4), scales=scales, in_=rounded.rearrange("p c t -> p (c t)"))

        def product(dst, lhs_codes, lhs_scales, rhs_codes, rhs_scales):
            nc.tensor.matmul_mx(
                out=dst, lhsT=lhs_codes.bitcast(FP8X4), lhsT_scale=lhs_scales,
                rhs=rhs_codes.bitcast(FP8X4), rhs_scale=rhs_scales, start=True, stop=True,
            )

        def scaled_copy(dst, src, scale):
            nc.scalar.activation(dst, src, ACT.Copy, scale=scale)

        offs_sb, n1_sb, n2_sb, n3_sb, n4_sb = [
            keep.tile([P, S // LIST_ROWS], U16, name=name) for name in ("offs_sb", "n1_sb", "n2_sb", "n3_sb", "n4_sb")
        ]
        x_scales_sb = keep.tile([P, T], U8, name="x_scales_sb", tag="x_scales_sb", align_bytes=64)
        x_words_sb = keep.tile([P, T], U32, name="x_words_sb", align_bytes=64)
        nc.gpsimd.memset(x_scales_sb[:].bitcast(I32), 0)

        nc.sync.dma_start(offs_sb[:], offs)
        wa_rows = wa.rearrange("(p j) c -> p j c", j=PACK)
        wa_raw = [keep.tile([P, PACK, HALF], F32, name=f"wa_raw{a}", tag=f"wa_raw{a}") for a in range(2)]
        nc.sync.dma_start(wa_raw[0][:], wa_rows[:, :, LEFT])
        for r in range(4):
            nc.sync.dma_start(x_scales_sb[r:P:32, :].bitcast(I32), x_scales[0, r:16:4, :].bitcast(I32))
        nc.sync.dma_start(x_words_sb[:].bitcast(I32), x_words[0].rearrange("p c r -> p (c r)").bitcast(I32))
        nc.sync.dma_start(wa_raw[1][:], wa_rows[:, :, RIGHT])
        gt_sb = keep.tile([P, PACK], F32, name="gt_sb")
        nc.sync.dma_start(gt_sb[:], gt.rearrange("(p t) o -> p (t o)", t=PACK))
        nc.sync.dma_start(n1_sb[:], n1)
        nc.sync.dma_start(n2_sb[:], n2)
        w1_raw = keep.tile([P, PACK, N], F32, name="w1_raw")
        nc.sync.dma_start(w1_raw[:], w1.rearrange("(p j) c -> p j c", j=PACK))
        nc.sync.dma_start(n3_sb[:], n3)
        nc.sync.dma_start(n4_sb[:], n4)

        window = [keep.tile([P, 2 * H], F32, name=f"window{t}") for t in range(PACK)]
        for t in range(PACK):
            nc.vector.memset(window[t][:, H:], 0.0)
        ident = keep.tile([P, P], F32, name="ident")
        make_identity(nc, ident[:])

        picked_scales = keep.tile([P, S], U8, name="picked_scales", align_bytes=64)
        picked_words = keep.tile([P, S], U32, name="picked_words", align_bytes=64)
        token_scales = keep.tile([P, S], U8, name="token_scales", align_bytes=64)
        token_words0 = keep.tile([P, P], U32, name="token_words0", align_bytes=64)
        wa_scales = keep.tile([P, H], U8, name="wa_scales", align_bytes=64)
        wa_bf = [keep.tile([P, HALF, PACK], BF16, name=f"wa_bf{a}", tag=f"wa_bf{a}", align_bytes=64) for a in range(2)]

        round_and_interleave(nc.scalar.copy, wa_bf[0][:], wa_raw[0][:])
        nc.vector.tensor_copy(picked_scales[:], x_scales_sb[:].indirect(offs_sb[:]))
        wa_codes = keep.tile([P, H], U32, name="wa_codes", tag="x_scales_sb", align_bytes=64)
        quantize(wa_codes[:, LEFT], wa_scales[:, LEFT], wa_bf[0][:])
        nc.vector.tensor_copy(
            token_scales[:].rearrange("p (t m) -> p t m", t=PACK), picked_scales[:].rearrange("p (m t) -> p t m", t=PACK)
        )
        nc.vector.tensor_copy(picked_words[:], x_words_sb[:].indirect(offs_sb[:]))
        picked_by_tile = picked_words[:].bitcast(I32).rearrange("p (m t) -> p t m", t=PACK)
        nc.vector.tensor_copy(token_words0[:].bitcast(I32), picked_by_tile[:, 0, :])
        round_shared(wa_bf[1][:], wa_raw[1][:], WA_VECTOR_COLS)
        quantize(wa_codes[:, RIGHT], wa_scales[:, RIGHT], wa_bf[1][:])
        token_words_rest = keep.tile([P, LAST, P], U32, name="token_words_rest", tag="wa_bf1", align_bytes=64)
        nc.vector.tensor_copy(token_words_rest[:].bitcast(I32), picked_by_tile[:, 1:, :])
        token_words = [token_words0[:]] + [token_words_rest[:, t, :] for t in range(LAST)]

        gt_safe = keep.tile([P, PACK], F32, name="gt_safe", tag="wa_raw1")
        gt_reciprocal = keep.tile([P, PACK], F32, name="gt_reciprocal")
        gt_inverse = keep.tile([P, PACK], F32, name="gt_inverse")
        nc.vector.scalar_tensor_tensor(gt_safe[:], gt_sb[:], 0.0, gt_sb[:], ALU.is_equal, ALU.add)
        nc.vector.reciprocal(gt_reciprocal[:], gt_safe[:])
        nc.vector.tensor_scalar(gt_inverse[:], gt_reciprocal[:], FINITE, -FINITE, ALU.min, ALU.max)

        bank = [psum.tile([P, H], F32, name=f"bank{b}") for b in range(8)]
        twin = [keep.tile([P, H], F32, name=f"twin{t}") for t in range(PACK)]
        y_twin = twin[:LAST] + [keep.tile([P, H], F32, name="y_twin_last", tag="y_twin_last", align_bytes=64)]
        gated_st = [keep.tile([P, H], F32, name=f"gated_st{t}") for t in range(PACK)]
        tanh_st = [keep.tile([P, H], F32, name=f"tanh_st{t}") for t in range(PACK)]

        def y_product(dst, t, cols):
            product(dst, token_words[t], token_scales[:, t * P : (t + 1) * P], wa_codes[:, cols], wa_scales[:, cols])

        def add_looked_up_y(t, cols):
            nc.vector.tensor_tensor(
                gated_st[t][:, cols], window[t][:].indirect(entries(n1_sb, cols)), y_twin[t][:, cols], ALU.add
            )

        y_halves = ((LEFT, bank[0][:, :HALF]), (RIGHT, bank[4][:, :HALF]))
        for cols, y_half in y_halves:
            y_product(y_half, 0, cols)
        for cols, y_half in y_halves:
            scaled_copy(window[0][:, cols], y_half, gt_sb[:, 0:1])
            scaled_copy(y_twin[0][:, cols], y_half, gt_sb[:, 0:1])
        for cols in (LEFT, RIGHT):
            add_looked_up_y(0, cols)
        for t in range(1, PACK):
            y_product(bank[t][:], t, WHOLE)
            scaled_copy(window[t][:, WHOLE], bank[t][:], gt_sb[:, t : t + 1])
            scaled_copy(y_twin[t][:], bank[t][:], gt_sb[:, t : t + 1])
            add_looked_up_y(t, WHOLE)
        for t in range(PACK):
            nc.scalar.activation(tanh_st[t][:], gated_st[t][:], ACT.Tanh, scale=gt_inverse[:, t : t + 1])

        w1_bf = keep.tile([P, PACK, P, PACK], BF16, name="w1_bf", tag="y_twin_last", align_bytes=64)
        w1_dst = w1_bf[:].rearrange("p t m j -> p m t j")
        w1_src = w1_raw[:].rearrange("p j (m t) -> p m t j", t=PACK)
        piece = P // W1_PIECES
        for q in range(W1_PIECES):
            nc.scalar.copy(w1_dst[:, q * piece : (q + 1) * piece], w1_src[:, q * piece : (q + 1) * piece])

        z = [keep.tile([P, PACK, HALF], F32, name=f"z{a}") for a in range(2)]
        for a, cols in enumerate((LEFT, RIGHT)):
            for t in range(PACK):
                nc.vector.tensor_tensor(
                    z[a][:, t, :], tanh_st[t][:].indirect(entries(n2_sb, cols)), gated_st[t][:, cols], ALU.mult
                )

        w1_codes0 = keep.tile([P, P], U32, name="w1_codes0", align_bytes=64)
        w1_scales = keep.tile([P, N], U8, name="w1_scales", align_bytes=64)
        w1_cols = w1_bf[:].rearrange("p t m j -> p (t m) j")
        quantize(w1_codes0[:], w1_scales[:, :P], w1_cols[:, :P, :])

        z_bf = [keep.tile([P, HALF, PACK], BF16, name=f"z_bf{a}", tag=f"z_bf{a}", align_bytes=64) for a in range(2)]
        z_codes = keep.tile([P, H], U32, name="z_codes", align_bytes=64)
        z_scales = keep.tile([P, H], U8, name="z_scales", align_bytes=64)
        round_and_interleave(nc.scalar.copy, z_bf[0][:], z[0][:])
        round_shared(z_bf[1][:], z[1][:], Z_VECTOR_COLS)

        def h_product(dst, codes, t, cols):
            product(dst, codes, w1_scales[:, t * P : (t + 1) * P], z_codes[:, cols], z_scales[:, cols])

        for a, cols in enumerate((LEFT, RIGHT)):
            quantize(z_codes[:, cols], z_scales[:, cols], z_bf[a][:])
            h_product(bank[a][:, :HALF], w1_codes0[:], 0, cols)
        w1_codes_rest = keep.tile([P, N - P], U32, name="w1_codes_rest", tag="z_bf1", align_bytes=64)
        quantize(w1_codes_rest[:, :P], w1_scales[:, P : 2 * P], w1_cols[:, P : 2 * P, :])
        quantize(w1_codes_rest[:, P:], w1_scales[:, 2 * P :], w1_cols[:, 2 * P :, :])
        scaled_copy(window[0][:, LEFT], bank[0][:, :HALF], 0.5)
        scaled_copy(twin[0][:, LEFT], bank[0][:, :HALF], 0.5)
        nc.vector.tensor_scalar(window[0][:, RIGHT], bank[1][:, :HALF], 0.5, None, ALU.mult)
        scaled_copy(twin[0][:, RIGHT], bank[1][:, :HALF], 0.5)
        for t in range(1, PACK):
            h_product(bank[4 + t][:], w1_codes_rest[:, (t - 1) * P : t * P], t, WHOLE)
            scaled_copy(window[t][:, WHOLE], bank[4 + t][:], 0.5)
            scaled_copy(twin[t][:], bank[4 + t][:], 0.5)

        out_rows = out.rearrange("(p t) j -> p t j", t=PACK)
        above = [keep.tile([P, H], F32, name=f"above{t}") for t in range(PACK)]
        below = [keep.tile([P, H], F32, name=f"below{t}") for t in range(PACK)]
        result = [keep.tile([P, H], F32, name=f"result{t}") for t in range(PACK)]
        da = [gated_st[(2 * t) % RING] for t in range(PACK)]
        db = [gated_st[(2 * t + 1) % RING] for t in range(PACK)]
        minus_below = keep.tile([P, H], F32, name="minus_below")

        def difference(dst, t, list_sb, cols):
            nc.vector.tensor_tensor(
                dst[:, cols], window[t][:].indirect(entries(list_sb, cols)), twin[t][:, cols], ALU.subtract
            )

        def extreme(dst, t, op, cols):
            nc.vector.scalar_tensor_tensor(dst[:, cols], da[t][:, cols], 0.0, db[t][:, cols], op, op)

        def sum_on_tensor_engine(t):
            turned = keep.tile([P, H], F32, name=f"turned{t}")
            scaled_copy(minus_below[:], below[t][:], -1.0)
            sums = [bank[b][:, :P] for b in (2, 3, 4, 0)]
            blocks = [slice(q * P, (q + 1) * P) for q in range(H // P)]
            for block_sum, block in zip(sums, blocks):
                for i, term in enumerate((twin[t], above[t], above[t])):
                    nc.tensor.matmul(block_sum, term[:, block], ident[:], start=(i == 0), stop=False, is_transpose=True)
            for block_sum, block in zip(sums, blocks):
                nc.tensor.matmul(block_sum, minus_below[:, block], ident[:], start=False, stop=True, is_transpose=True)
                nc.scalar.copy(turned[:, block], block_sum)
            for a, (cols, back) in enumerate(((LEFT, bank[1]), (RIGHT, bank[5]))):
                for q in range(2):
                    nc.tensor.transpose(back[:, blocks[q]], turned[:, blocks[2 * a + q]], ident[:])
                nc.scalar.copy(result[t][:, cols], back[:, :HALF])
                nc.sync.dma_start(out_rows[:, t, cols], result[t][:, cols])

        for cols in (LEFT, RIGHT):
            difference(da[0], 0, n3_sb, cols)
        for t in range(LAST):
            difference(db[t], t, n4_sb, WHOLE)
            difference(da[t + 1], t + 1, n3_sb, WHOLE)
            extreme(above[t], t, ALU.max, WHOLE)
            extreme(below[t], t, ALU.min, WHOLE)
            sum_on_tensor_engine(t)

        upper = keep.tile([P, H], F32, name="upper")
        for cols in (LEFT, RIGHT):
            difference(db[LAST], LAST, n4_sb, cols)
        for cols in (LEFT, RIGHT):
            extreme(above[LAST], LAST, ALU.max, cols)
            extreme(below[LAST], LAST, ALU.min, cols)
        for cols in (LEFT, RIGHT):
            nc.vector.scalar_tensor_tensor(
                upper[:, cols], above[LAST][:, cols], 2.0, twin[LAST][:, cols], ALU.mult, ALU.add
            )
        for cols in (LEFT, RIGHT):
            nc.vector.tensor_tensor(result[LAST][:, cols], upper[:, cols], below[LAST][:, cols], ALU.subtract)
            nc.sync.dma_start(out_rows[:, LAST, cols], result[LAST][:, cols])
